import numpy as np
import ml_dtypes


def mxq(x, axis, fmt="e4m3"):
    dtype, down = {"e4m3": (ml_dtypes.float8_e4m3fn, 7), "e5m2": (ml_dtypes.float8_e5m2, 14)}[fmt]
    v = np.moveaxis(np.asarray(x, np.float32).astype(ml_dtypes.bfloat16).astype(np.float64), axis, -1)
    blocks = v.reshape(v.shape[:-1] + (-1, 32))
    amax = np.abs(blocks).max(-1, keepdims=True)
    byte = np.maximum(np.where(amax > 0, np.frexp(amax)[1] - 1 + 127, 0) - down, 1)
    scale = np.exp2(byte - 127.0)
    codes = (blocks / scale).astype(np.float32).astype(dtype).astype(np.float64)
    return np.moveaxis((codes * scale).reshape(v.shape), -1, axis)


WIDE = False


def mx_kscale(k):
    if not WIDE:
        return np.ones(k)
    levels = np.array([10, -10, 5, -5, 0])
    if k % 512:
        return np.exp2(np.random.permutation(np.resize(levels, k // 32))).repeat(32)
    a = np.empty((k // 512, 16))
    for p in range(k // 512):
        a[p, :8] = np.random.permutation(np.resize(levels, 8))
        for g in range(8):
            far = levels[np.abs(levels - a[p, g]) >= 10]
            a[p, g + 8] = far[np.random.randint(len(far))]
    return np.exp2(a.ravel()).repeat(32)


def f64(x):
    return np.asarray(x).astype(np.float64)


def striped8(idx):
    return np.asarray(idx).reshape(8, -1, 16).transpose(0, 2, 1).reshape(128, -1).astype(np.uint16)


def unstriped8(offs):
    return offs.reshape(8, 16, -1).transpose(0, 2, 1).reshape(8, -1).astype(np.int64)


def pick8(x, idx, run):
    r = np.arange(len(x))
    return x[r[:, None], idx[r % (8 * run) // run]]


E2M1 = np.array([0.0, 0.5, 1.0, 1.5, 2.0, 3.0, 4.0, 6.0, -0.0, -0.5, -1.0, -1.5, -2.0, -3.0, -4.0, -6.0])


def pack_weight(w, fmt):
    k, n = w.shape
    w = f64(np.asarray(w, np.float32).astype(ml_dtypes.bfloat16)).reshape(k // 32, 32, n)
    amax = np.abs(w).max(1)
    if fmt == "e4m3":
        byte = np.frexp(amax)[1] - 1 + 127 - 7
    else:
        mant, ex = np.frexp(amax / 6.0)
        byte = np.where(mant > 0.5, ex, ex - 1) + 127
    byte = np.clip(np.where(amax > 0, byte, 1), 1, 254)
    scaled = (w * np.exp2(127.0 - byte)[:, None, :]).reshape(k, n).astype(np.float32)
    by_word = np.ascontiguousarray(scaled.reshape(k // 512, 128, 4, n).transpose(0, 1, 3, 2))
    if fmt == "e4m3":
        words = by_word.astype(ml_dtypes.float8_e4m3fn).view(np.uint8)
    else:
        c = by_word.astype(ml_dtypes.float4_e2m1fn).view(np.uint8) & 0xF
        words = (c[..., 0::2] | (c[..., 1::2] << 4)).reshape(k // 512, 128, 2 * n)
    return np.ascontiguousarray(words), np.ascontiguousarray(byte.astype(np.uint8).reshape(k // 512, 16, n))


def unpack_weight(words, scales, fmt):
    g, _, n = scales.shape
    words = np.ascontiguousarray(words).reshape(g, 128, n, -1)
    if fmt == "e4m3":
        vals = words.view(ml_dtypes.float8_e4m3fn).astype(np.float64)
    else:
        nib = np.empty((g, 128, n, 4), np.uint8)
        nib[..., 0::2] = words & 0xF
        nib[..., 1::2] = words >> 4
        vals = E2M1[nib]
    vals = vals * np.repeat(np.exp2(scales.astype(np.float64) - 127.0), 8, axis=1)[..., None]
    return vals.transpose(0, 1, 3, 2).reshape(g * 512, n)


D, T, U, X, S, I, J, Q = 512, 1024, 1024, 1024, 1024, 512, 256, 128


def setup_inputs():
    n = np.random.standard_normal
    idx = np.stack([np.random.permutation(T)[:J] for _ in range(8)])
    idx2 = np.stack([np.random.permutation(U)[:J] for _ in range(8)])
    idx3 = np.stack([np.random.permutation(X)[:J] for _ in range(8)])
    idx4 = np.stack([np.random.permutation(S)[:J] for _ in range(8)])
    idx5 = np.stack([np.random.permutation(T)[:I] for _ in range(8)])
    idx6 = np.stack([np.random.permutation(U)[:I] for _ in range(8)])
    idx7 = np.stack([np.random.permutation(T)[:I] for _ in range(8)])
    idx8 = np.stack([np.random.permutation(U)[:I] for _ in range(8)])
    fd = mx_kscale(D)
    cachep = pack_weight(n((D, T)) / fd[:, None], "e4m3")
    draftp = pack_weight(n((D, U)) / fd[:, None], "e2m1")
    archp = pack_weight(n((D, X)) / fd[:, None], "e4m3")
    prefp = pack_weight(n((D, S)) / fd[:, None], "e2m1")
    return {
        "query": (n((D, Q)) * 1.0 / np.sqrt(D) * fd[:, None]).astype(np.float32),
        "cache_words": cachep[0],
        "cache_scales": cachep[1],
        "draft_words": draftp[0],
        "draft_scales": draftp[1],
        "arch_words": archp[0],
        "arch_scales": archp[1],
        "pref_words": prefp[0],
        "pref_scales": prefp[1],
        "offs": striped8(idx),
        "offs2": striped8(idx2),
        "offs3": striped8(idx3),
        "offs4": striped8(idx4),
        "offs5": striped8(idx5),
        "offs6": striped8(idx6),
        "offs7": striped8(idx7),
        "offs8": striped8(idx8),
    }


def reference(query, cache_words, cache_scales, draft_words, draft_scales, arch_words, arch_scales, pref_words, pref_scales, offs, offs2, offs3, offs4, offs5, offs6, offs7, offs8):
    idx = unstriped8(offs)
    idx2 = unstriped8(offs2)
    idx3 = unstriped8(offs3)
    idx4 = unstriped8(offs4)
    idx5 = unstriped8(offs5)
    idx6 = unstriped8(offs6)
    idx7 = unstriped8(offs7)
    idx8 = unstriped8(offs8)
    cacheu = unpack_weight(cache_words, cache_scales, "e4m3")
    draftu = unpack_weight(draft_words, draft_scales, "e2m1")
    archu = unpack_weight(arch_words, arch_scales, "e4m3")
    prefu = unpack_weight(pref_words, pref_scales, "e2m1")
    queryq = mxq(f64(query), 0, "e4m3")
    a = queryq.T @ cacheu
    b = queryq.T @ draftu
    c0 = queryq.T @ archu
    d0 = queryq.T @ prefu
    hi1 = np.maximum(pick8(a, idx, 16), pick8(b, idx2, 16))
    lo1 = np.minimum(pick8(c0, idx3, 16), pick8(d0, idx4, 16))
    w = np.concatenate([hi1, lo1], axis=1)
    f1 = np.zeros((Q, T))
    f1[np.arange(Q)[:, None], idx5[np.arange(Q) % 128 // 16]] = w
    f2 = np.zeros((Q, U))
    f2[np.arange(Q)[:, None], idx6[np.arange(Q) % 128 // 16]] = w
    aa = a - f1
    bb = b + f2
    y = np.minimum(pick8(aa, idx7, 16), pick8(bb, idx8, 16))
    return y

@@ -1,0 +1,176 @@
+from contextlib import ExitStack
+
+import concourse.mybir as mybir
+
+F32 = mybir.dt.float32
+BF16 = mybir.dt.bfloat16
+I32 = mybir.dt.int32
+U32 = mybir.dt.uint32
+U16 = mybir.dt.uint16
+U8 = mybir.dt.uint8
+FP8X4 = mybir.dt.float8_e4m3fn_x4
+FP4X4 = mybir.dt.float4_e2m1fn_x4
+ALU = mybir.AluOpType
+COPY = mybir.ActivationFunctionType.Copy
+
+P = 128
+PACK = 4
+Q = 128
+T = 1024
+PICKS = 256
+SLOTS = 512
+BANK = 512
+FP8_ROW = 4
+FLOPS = 4 * 2 * 512 * Q * T
+
+
+def tile_attend_fourcourts_four_kernel(tc, query, cache_words, cache_scales, draft_words, draft_scales,
+                                        arch_words, arch_scales, pref_words, pref_scales,
+                                        offs, offs2, offs3, offs4, offs5, offs6, offs7, offs8, out):
+    nc = tc.nc
+    with ExitStack() as ctx:
+        sb = ctx.enter_context(tc.tile_pool(name="sb", bufs=1))
+        ps = ctx.enter_context(tc.psum_pool(name="ps", bufs=1))
+
+        def scale_tile(name):
+            t = sb.tile([P, 2 * T], U8, name=name, align_bytes=64)
+            nc.vector.memset(t[:].bitcast(I32)[0:64, :], 0)
+            return t
+
+        def load_scales(t, scales, row):
+            src = scales[0].bitcast(I32).rearrange("(h u r) n -> u r h n", h=2, u=2, r=4)
+            dst = t[:].bitcast(I32).rearrange("p (h n) -> p h n", h=2)
+            for u in range(2):
+                nc.sync.dma_start(out=dst[32 * u + row:32 * u + row + 4], in_=src[u])
+
+        def spread_scales(t):
+            w = t[:].bitcast(I32)
+            nc.vector.tensor_copy(out=w[64:128, 0:T // 4], in_=w[0:64, T // 4:T // 2])
+
+        def load_list(src, name):
+            t = sb.tile([P, src.shape[1]], U16, name=name)
+            nc.sync.dma_start(t[:], src)
+            return t
+
+        def load_fp8(words, lo, hi, name):
+            t = sb.tile([P, hi - lo], U32, name=name, align_bytes=64)
+            src = words[0].rearrange("p n t -> p (n t)")[:, 4 * lo:4 * hi].bitcast(I32)
+            nc.sync.dma_start(out=t[:].bitcast(I32), in_=src)
+            return t
+
+        def load_fp4(words, name):
+            t = sb.tile([P, 2 * T], U8, name=name, align_bytes=64)
+            nc.sync.dma_start(out=t[:].bitcast(I32), in_=words[0].bitcast(I32))
+            return t
+
+        b_sc = scale_tile("b_sc")
+        a_sc = scale_tile("a_sc")
+        c_sc = scale_tile("c_sc")
+        d_sc = scale_tile("d_sc")
+        f1 = sb.tile([P, T], F32)
+        f2 = sb.tile([P, T], F32)
+        nc.vector.memset(f1[:], 0.0)
+        nc.gpsimd.memset(f2[:], 0.0)
+
+        q_raw = sb.tile([P, PACK, Q], F32)
+        nc.sync.dma_start(out=q_raw[:], in_=query.rearrange("(p j) w -> p j w", j=PACK))
+        load_scales(b_sc, draft_scales, 0)
+        b_w = load_fp4(draft_words, "b_w")
+        load_scales(a_sc, cache_scales, FP8_ROW)
+        l2 = load_list(offs2, "l2")
+        a_w = load_fp8(cache_words, 0, T, "a_w")
+        load_scales(c_sc, arch_scales, FP8_ROW)
+        c_w = load_fp8(arch_words, 0, T, "c_w")
+        d_w = load_fp4(pref_words, "d_w")
+        load_scales(d_sc, pref_scales, 0)
+        l1 = load_list(offs, "l1")
+        l5 = load_list(offs5, "l5")
+        l3 = load_list(offs3, "l3")
+        l4 = load_list(offs4, "l4")
+        l6 = load_list(offs6, "l6")
+        l7 = load_list(offs7, "l7")
+        l8 = load_list(offs8, "l8")
+
+        q_bf = sb.tile([P, Q, PACK], BF16, align_bytes=64)
+        q_by_col = q_raw[:].rearrange("p j w -> p w j")
+        half = Q // 2
+        nc.scalar.activation(out=q_bf[:, 0:half, :], in_=q_by_col[:, 0:half, :], func=COPY)
+        spread_scales(b_sc)
+        nc.vector.tensor_copy(out=q_bf[:, half:Q, :], in_=q_by_col[:, half:Q, :])
+        q_codes = sb.tile([P, Q], U32, align_bytes=64)
+        q_sc = sb.tile([P, Q], U8, align_bytes=64)
+        nc.vector.quantize_mx(out=q_codes[:].bitcast(FP8X4), scales=q_sc[:], in_=q_bf[:].rearrange("p w j -> p (w j)"))
+        spread_scales(a_sc)
+        spread_scales(c_sc)
+        spread_scales(d_sc)
+
+        def score(bank, rhs, rhs_scale):
+            nc.tensor.matmul_mx(out=bank, lhsT=q_codes[:].bitcast(FP8X4), lhsT_scale=q_sc[:],
+                                rhs=rhs, rhs_scale=rhs_scale, start=True, stop=True)
+
+        def score_fp4(tag, words, sc, lo, hi):
+            bank = ps.tile([P, BANK], F32, name=tag, tag=tag)
+            score(bank[:, 0:hi - lo], words[:, 2 * lo:2 * hi].bitcast(FP4X4), sc[:, lo:hi])
+            return bank[:, 0:hi - lo]
+
+        def score_fp8(tag, words, base, sc, lo, hi):
+            bank = ps.tile([P, BANK], F32, name=tag, tag=tag)
+            score(bank[:, 0:hi - lo], words[:, lo - base:hi - base].bitcast(FP8X4), sc[FP8_ROW:P, lo:hi])
+            return bank[:, 0:hi - lo]
+
+        a = sb.tile([P, T], F32)
+        b = sb.tile([P, T], F32)
+        c = sb.tile([P, T], F32)
+        d = sb.tile([P, T], F32)
+        mid = BANK + BANK // 2
+        pb0 = score_fp4("bank0", b_w, b_sc, 0, BANK)
+        pb1 = score_fp4("bank1", b_w, b_sc, BANK, T)
+        pa0 = score_fp8("bank2", a_w, 0, a_sc, 0, BANK)
+        pa1 = score_fp8("bank3", a_w, 0, a_sc, BANK, mid)
+        pa2 = score_fp8("bank4", a_w, 0, a_sc, mid, T)
+        nc.scalar.copy(out=b[:, 0:BANK], in_=pb0)
+        nc.scalar.copy(out=b[:, BANK:T], in_=pb1)
+        nc.vector.tensor_copy(out=a[:, 0:BANK], in_=pa0)
+        gb = sb.tile([P, PICKS], F32)
+        nc.scalar.activation(out=gb[:], in_=b[:].indirect(l2[:]), func=COPY)
+        nc.vector.tensor_copy(out=a[:, BANK:mid], in_=pa1)
+        nc.scalar.copy(out=a[:, mid:T], in_=pa2)
+        ga = sb.tile([P, PICKS], F32)
+        nc.scalar.activation(out=ga[:], in_=a[:].indirect(l1[:]), func=COPY)
+        hi1 = sb.tile([P, PICKS], F32)
+        nc.vector.tensor_tensor(out=hi1[:], in0=ga[:], in1=gb[:], op=ALU.max)
+
+        pc0 = score_fp8("bank5", c_w, 0, c_sc, 0, BANK)
+        pc1 = score_fp8("bank6", c_w, 0, c_sc, BANK, T)
+        pd0 = score_fp4("bank7", d_w, d_sc, 0, BANK)
+        pd1 = score_fp4("bank2", d_w, d_sc, BANK, T)
+        nc.vector.tensor_copy(out=c[:, 0:BANK], in_=pc0)
+        cols = PICKS // 16
+        nc.scalar.activation(out=f1[:].indirect(l5[:, 0:cols]), in_=hi1[:], func=COPY)
+        nc.scalar.activation(out=f2[:].indirect(l6[:, 0:cols]), in_=hi1[:], func=COPY)
+        nc.vector.tensor_copy(out=c[:, BANK:T], in_=pc1)
+        gc = sb.tile([P, PICKS], F32)
+        nc.vector.tensor_copy(out=gc[:], in_=c[:].indirect(l3[:]))
+        nc.vector.tensor_copy(out=d[:, 0:BANK], in_=pd0)
+        nc.vector.tensor_copy(out=d[:, BANK:T], in_=pd1)
+        gd = sb.tile([P, PICKS], F32)
+        nc.vector.tensor_copy(out=gd[:], in_=d[:].indirect(l4[:]))
+        lo1 = sb.tile([P, PICKS], F32)
+        nc.vector.tensor_tensor(out=lo1[:], in0=gc[:], in1=gd[:], op=ALU.min)
+        nc.scalar.activation(out=f1[:].indirect(l5[:, cols:2 * cols]), in_=lo1[:], func=COPY)
+        nc.scalar.activation(out=f2[:].indirect(l6[:, cols:2 * cols]), in_=lo1[:], func=COPY)
+
+        aa = sb.tile([P, T], F32)
+        bb = sb.tile([P, T], F32)
+        nc.vector.tensor_tensor(out=aa[:], in0=a[:], in1=f1[:], op=ALU.subtract)
+        g7 = [sb.tile([P, PICKS], F32, name="g7_%d" % h) for h in range(2)]
+        g8 = [sb.tile([P, PICKS], F32, name="g8_%d" % h) for h in range(2)]
+        nc.vector.tensor_copy(out=g7[0][:], in_=aa[:].indirect(l7[:, 0:cols]))
+        nc.scalar.activation(out=g7[1][:], in_=aa[:].indirect(l7[:, cols:2 * cols]), func=COPY)
+        nc.vector.tensor_tensor(out=bb[:], in0=b[:], in1=f2[:], op=ALU.add)
+        nc.vector.tensor_copy(out=g8[0][:], in_=bb[:].indirect(l8[:, 0:cols]))
+        nc.scalar.activation(out=g8[1][:], in_=bb[:].indirect(l8[:, cols:2 * cols]), func=COPY)
+        for h, queue in enumerate((nc.sync, nc.scalar)):
+            y = sb.tile([P, PICKS], F32, name="y%d" % h)
+            nc.vector.tensor_tensor(out=y[:], in0=g7[h][:], in1=g8[h][:], op=ALU.min)
+            queue.dma_start(out=out[:, h * PICKS:(h + 1) * PICKS], in_=y[:])

@@ -15,13 +15,19 @@ COPY = mybir.ActivationFunctionType.Copy
 
 P = 128
 PACK = 4
+D = P * PACK
 Q = 128
 T = 1024
 PICKS = 256
-SLOTS = 512
 BANK = 512
-FP8_ROW = 4
-FLOPS = 4 * 2 * 512 * Q * T
+QUAD = 32
+ROWS = 4
+PER_COL = 16
+FP8_FIRST = 4
+TAIL = T - BANK // 2
+LEAD = T // 16
+
+FLOPS = 4 * 2 * D * Q * T
 
 
 def tile_attend_fourcourts_four_kernel(tc, query, cache_words, cache_scales, draft_words, draft_scales,
@@ -32,145 +38,151 @@ def tile_attend_fourcourts_four_kernel(tc, query, cache_words, cache_scales, dra
         sb = ctx.enter_context(tc.tile_pool(name="sb", bufs=1))
         ps = ctx.enter_context(tc.psum_pool(name="ps", bufs=1))
 
-        def scale_tile(name):
-            t = sb.tile([P, 2 * T], U8, name=name, align_bytes=64)
-            nc.vector.memset(t[:].bitcast(I32)[0:64, :], 0)
-            return t
-
-        def load_scales(t, scales, row):
-            src = scales[0].bitcast(I32).rearrange("(h u r) n -> u r h n", h=2, u=2, r=4)
-            dst = t[:].bitcast(I32).rearrange("p (h n) -> p h n", h=2)
+        def load_folded_plane(plane, scales, first):
+            src = scales[0].bitcast(I32).rearrange("(h u r) n -> u r h n", h=2, u=2, r=ROWS)
+            dst = plane[:].bitcast(I32).rearrange("p (h n) -> p h n", h=2)
             for u in range(2):
-                nc.sync.dma_start(out=dst[32 * u + row:32 * u + row + 4], in_=src[u])
+                nc.sync.dma_start(out=dst[QUAD * u + first:QUAD * u + first + ROWS], in_=src[u])
 
-        def spread_scales(t):
-            w = t[:].bitcast(I32)
-            nc.vector.tensor_copy(out=w[64:128, 0:T // 4], in_=w[0:64, T // 4:T // 2])
+        def unfold_plane(plane):
+            as_i32 = plane[:].bitcast(I32)
+            nc.vector.tensor_copy(out=as_i32[P // 2:P, 0:T // 4], in_=as_i32[0:P // 2, T // 4:T // 2])
+
+        def load_direct_plane(plane, scales, first, queue):
+            src = scales[0].bitcast(I32).rearrange("(u r) n -> r u n", r=ROWS)
+            for r in range(ROWS):
+                queue.dma_start(out=plane[:].bitcast(I32)[first + r:P:QUAD, :], in_=src[r])
 
         def load_list(src, name):
-            t = sb.tile([P, src.shape[1]], U16, name=name)
-            nc.sync.dma_start(t[:], src)
-            return t
+            entries = sb.tile([P, src.shape[1]], U16, name=name)
+            nc.sync.dma_start(entries[:], src)
+            return entries
 
-        def load_fp8(words, lo, hi, name):
-            t = sb.tile([P, hi - lo], U32, name=name, align_bytes=64)
-            src = words[0].rearrange("p n t -> p (n t)")[:, 4 * lo:4 * hi].bitcast(I32)
-            nc.sync.dma_start(out=t[:].bitcast(I32), in_=src)
-            return t
+        def load_fp8_words(words, name):
+            codes = sb.tile([P, T], U32, name=name, align_bytes=64)
+            nc.sync.dma_start(out=codes[:].bitcast(I32), in_=words[0].rearrange("p n t -> p (n t)").bitcast(I32))
+            return codes
 
-        def load_fp4(words, name):
-            t = sb.tile([P, 2 * T], U8, name=name, align_bytes=64)
-            nc.sync.dma_start(out=t[:].bitcast(I32), in_=words[0].bitcast(I32))
-            return t
+        def load_fp4_words(words, name):
+            codes = sb.tile([P, 2 * T], U8, name=name, align_bytes=64)
+            nc.sync.dma_start(out=codes[:].bitcast(I32), in_=words[0].bitcast(I32))
+            return codes
 
-        b_sc = scale_tile("b_sc")
-        a_sc = scale_tile("a_sc")
-        c_sc = scale_tile("c_sc")
-        d_sc = scale_tile("d_sc")
+        draft_plane = sb.tile([P, 2 * T], U8, align_bytes=64)
+        cache_plane = sb.tile([P, 2 * T], U8, align_bytes=64)
+        pref_plane = sb.tile([P, T], U8, align_bytes=64)
+        arch_plane = sb.tile([P, T], U8, align_bytes=64)
         f1 = sb.tile([P, T], F32)
-        f2 = sb.tile([P, T], F32)
+        nc.vector.memset(draft_plane[:].bitcast(I32)[0:P // 2, :], 0)
+        nc.vector.memset(cache_plane[:].bitcast(I32)[0:P // 2, 0:T // 4], 0)
+        nc.gpsimd.memset(cache_plane[:].bitcast(I32)[0:P // 2, T // 4:T // 2], 0)
+        nc.gpsimd.memset(arch_plane[:].bitcast(I32), 0)
+        nc.vector.memset(pref_plane[:].bitcast(I32), 0)
         nc.vector.memset(f1[:], 0.0)
+
+        load_direct_plane(arch_plane, arch_scales, FP8_FIRST, nc.gpsimd)
+        q_raw = sb.tile([P, PACK, Q], F32)
+        nc.sync.dma_start(out=q_raw[:], in_=query.rearrange("(p t) w -> p t w", t=PACK))
+        draft_codes = load_fp4_words(draft_words, "draft_codes")
+        load_folded_plane(draft_plane, draft_scales, 0)
+        idx2 = load_list(offs2, "idx2")
+        load_folded_plane(cache_plane, cache_scales, FP8_FIRST)
+        cache_codes = load_fp8_words(cache_words, "cache_codes")
+        pref_codes = load_fp4_words(pref_words, "pref_codes")
+        load_direct_plane(pref_plane, pref_scales, 0, nc.sync)
+        idx = load_list(offs, "idx")
+        arch_codes = load_fp8_words(arch_words, "arch_codes")
+        idx5 = load_list(offs5, "idx5")
+        idx4 = load_list(offs4, "idx4")
+        idx6 = load_list(offs6, "idx6")
+        idx3 = load_list(offs3, "idx3")
+        idx7 = load_list(offs7, "idx7")
+        idx8 = load_list(offs8, "idx8")
+
+        q_bf = sb.tile([P, Q, PACK], BF16, tag="q_bf_then_f2", align_bytes=64)
+        q_by_col = q_raw[:].rearrange("p t w -> p w t")
+        nc.scalar.activation(out=q_bf[:, 0:Q // 2, :], in_=q_by_col[:, 0:Q // 2, :], func=COPY)
+        nc.vector.tensor_copy(out=q_bf[:, Q // 2:Q, :], in_=q_by_col[:, Q // 2:Q, :])
+        unfold_plane(draft_plane)
+        q_codes = sb.tile([P, Q], U32, align_bytes=64)
+        q_plane = sb.tile([P, Q], U8, align_bytes=64)
+        nc.vector.quantize_mx(out=q_codes[:].bitcast(FP8X4), scales=q_plane[:],
+                              in_=q_bf[:].rearrange("p w t -> p (w t)"))
+        unfold_plane(cache_plane)
+        f2 = sb.tile([P, T], F32, tag="q_bf_then_f2", align_bytes=64)
         nc.gpsimd.memset(f2[:], 0.0)
 
-        q_raw = sb.tile([P, PACK, Q], F32)
-        nc.sync.dma_start(out=q_raw[:], in_=query.rearrange("(p j) w -> p j w", j=PACK))
-        load_scales(b_sc, draft_scales, 0)
-        b_w = load_fp4(draft_words, "b_w")
-        load_scales(a_sc, cache_scales, FP8_ROW)
-        l2 = load_list(offs2, "l2")
-        a_w = load_fp8(cache_words, 0, T, "a_w")
-        load_scales(c_sc, arch_scales, FP8_ROW)
-        c_w = load_fp8(arch_words, 0, T, "c_w")
-        d_w = load_fp4(pref_words, "d_w")
-        load_scales(d_sc, pref_scales, 0)
-        l1 = load_list(offs, "l1")
-        l5 = load_list(offs5, "l5")
-        l3 = load_list(offs3, "l3")
-        l4 = load_list(offs4, "l4")
-        l6 = load_list(offs6, "l6")
-        l7 = load_list(offs7, "l7")
-        l8 = load_list(offs8, "l8")
+        def score(bank_tag, keys, key_scales):
+            bank = ps.tile([P, BANK], F32, name=bank_tag, tag=bank_tag)
+            scores = bank[:, 0:key_scales.shape[1]]
+            nc.tensor.matmul_mx(out=scores, lhsT=q_codes[:].bitcast(FP8X4), lhsT_scale=q_plane[:],
+                                rhs=keys, rhs_scale=key_scales, start=True, stop=True)
+            return scores
 
-        q_bf = sb.tile([P, Q, PACK], BF16, align_bytes=64)
-        q_by_col = q_raw[:].rearrange("p j w -> p w j")
-        half = Q // 2
-        nc.scalar.activation(out=q_bf[:, 0:half, :], in_=q_by_col[:, 0:half, :], func=COPY)
-        spread_scales(b_sc)
-        nc.vector.tensor_copy(out=q_bf[:, half:Q, :], in_=q_by_col[:, half:Q, :])
-        q_codes = sb.tile([P, Q], U32, align_bytes=64)
-        q_sc = sb.tile([P, Q], U8, align_bytes=64)
-        nc.vector.quantize_mx(out=q_codes[:].bitcast(FP8X4), scales=q_sc[:], in_=q_bf[:].rearrange("p w j -> p (w j)"))
-        spread_scales(a_sc)
-        spread_scales(c_sc)
-        spread_scales(d_sc)
+        def score_fp4(bank_tag, codes, plane, lo, hi):
+            return score(bank_tag, codes[:, 2 * lo:2 * hi].bitcast(FP4X4), plane[:, lo:hi])
 
-        def score(bank, rhs, rhs_scale):
-            nc.tensor.matmul_mx(out=bank, lhsT=q_codes[:].bitcast(FP8X4), lhsT_scale=q_sc[:],
-                                rhs=rhs, rhs_scale=rhs_scale, start=True, stop=True)
-
-        def score_fp4(tag, words, sc, lo, hi):
-            bank = ps.tile([P, BANK], F32, name=tag, tag=tag)
-            score(bank[:, 0:hi - lo], words[:, 2 * lo:2 * hi].bitcast(FP4X4), sc[:, lo:hi])
-            return bank[:, 0:hi - lo]
-
-        def score_fp8(tag, words, base, sc, lo, hi):
-            bank = ps.tile([P, BANK], F32, name=tag, tag=tag)
-            score(bank[:, 0:hi - lo], words[:, lo - base:hi - base].bitcast(FP8X4), sc[FP8_ROW:P, lo:hi])
-            return bank[:, 0:hi - lo]
+        def score_fp8(bank_tag, codes, plane, lo, hi):
+            return score(bank_tag, codes[:, lo:hi].bitcast(FP8X4), plane[FP8_FIRST:P, lo:hi])
 
         a = sb.tile([P, T], F32)
         b = sb.tile([P, T], F32)
-        c = sb.tile([P, T], F32)
-        d = sb.tile([P, T], F32)
-        mid = BANK + BANK // 2
-        pb0 = score_fp4("bank0", b_w, b_sc, 0, BANK)
-        pb1 = score_fp4("bank1", b_w, b_sc, BANK, T)
-        pa0 = score_fp8("bank2", a_w, 0, a_sc, 0, BANK)
-        pa1 = score_fp8("bank3", a_w, 0, a_sc, BANK, mid)
-        pa2 = score_fp8("bank4", a_w, 0, a_sc, mid, T)
-        nc.scalar.copy(out=b[:, 0:BANK], in_=pb0)
-        nc.scalar.copy(out=b[:, BANK:T], in_=pb1)
-        nc.vector.tensor_copy(out=a[:, 0:BANK], in_=pa0)
-        gb = sb.tile([P, PICKS], F32)
-        nc.scalar.activation(out=gb[:], in_=b[:].indirect(l2[:]), func=COPY)
-        nc.vector.tensor_copy(out=a[:, BANK:mid], in_=pa1)
-        nc.scalar.copy(out=a[:, mid:T], in_=pa2)
-        ga = sb.tile([P, PICKS], F32)
-        nc.scalar.activation(out=ga[:], in_=a[:].indirect(l1[:]), func=COPY)
+        b_lo = score_fp4("bank0", draft_codes, draft_plane, 0, BANK)
+        b_mid = score_fp4("bank1", draft_codes, draft_plane, BANK, TAIL)
+        b_tail = score_fp4("bank2", draft_codes, draft_plane, TAIL, T)
+        a_lo = score_fp8("bank3", cache_codes, cache_plane, 0, BANK)
+        a_mid = score_fp8("bank4", cache_codes, cache_plane, BANK, TAIL)
+        a_tail = score_fp8("bank5", cache_codes, cache_plane, TAIL, T)
+        nc.scalar.copy(out=b[:, 0:BANK], in_=b_lo)
+        nc.vector.tensor_copy(out=b[:, BANK:TAIL], in_=b_mid)
+        nc.vector.tensor_copy(out=b[:, TAIL:T], in_=b_tail)
+        b_picks = sb.tile([P, PICKS], F32)
+        nc.vector.tensor_copy(out=b_picks[:], in_=b[:].indirect(idx2[:]))
+        nc.scalar.copy(out=a[:, 0:BANK], in_=a_lo)
+        nc.scalar.copy(out=a[:, BANK:TAIL], in_=a_mid)
+        nc.vector.tensor_copy(out=a[:, TAIL:T], in_=a_tail)
+        a_picks = sb.tile([P, PICKS], F32, tag="a_picks_then_d0_picks")
+        nc.vector.tensor_copy(out=a_picks[:], in_=a[:].indirect(idx[:]))
         hi1 = sb.tile([P, PICKS], F32)
-        nc.vector.tensor_tensor(out=hi1[:], in0=ga[:], in1=gb[:], op=ALU.max)
+        pieces = ((0, LEAD), (LEAD, PICKS))
+        for lo, hi in pieces:
+            nc.vector.tensor_tensor(out=hi1[:, lo:hi], in0=a_picks[:, lo:hi], in1=b_picks[:, lo:hi], op=ALU.max)
 
-        pc0 = score_fp8("bank5", c_w, 0, c_sc, 0, BANK)
-        pc1 = score_fp8("bank6", c_w, 0, c_sc, BANK, T)
-        pd0 = score_fp4("bank7", d_w, d_sc, 0, BANK)
-        pd1 = score_fp4("bank2", d_w, d_sc, BANK, T)
-        nc.vector.tensor_copy(out=c[:, 0:BANK], in_=pc0)
-        cols = PICKS // 16
-        nc.scalar.activation(out=f1[:].indirect(l5[:, 0:cols]), in_=hi1[:], func=COPY)
-        nc.scalar.activation(out=f2[:].indirect(l6[:, 0:cols]), in_=hi1[:], func=COPY)
-        nc.vector.tensor_copy(out=c[:, BANK:T], in_=pc1)
-        gc = sb.tile([P, PICKS], F32)
-        nc.vector.tensor_copy(out=gc[:], in_=c[:].indirect(l3[:]))
-        nc.vector.tensor_copy(out=d[:, 0:BANK], in_=pd0)
-        nc.vector.tensor_copy(out=d[:, BANK:T], in_=pd1)
-        gd = sb.tile([P, PICKS], F32)
-        nc.vector.tensor_copy(out=gd[:], in_=d[:].indirect(l4[:]))
+        d0 = sb.tile([P, T], F32, tag="d0_then_c0")
+        d0_lo = score_fp4("bank6", pref_codes, pref_plane, 0, BANK)
+        d0_hi = score_fp4("bank7", pref_codes, pref_plane, BANK, T)
+        c0_lo = score_fp8("bank3", arch_codes, arch_plane, 0, BANK)
+        c0_hi = score_fp8("bank4", arch_codes, arch_plane, BANK, T)
+        nc.scalar.copy(out=d0[:, 0:BANK], in_=d0_lo)
+        nc.scalar.copy(out=d0[:, BANK:T], in_=d0_hi)
+        half = PICKS // PER_COL
+        for lo, hi in pieces:
+            nc.scalar.activation(out=f1[:].indirect(idx5[:, lo // PER_COL:hi // PER_COL]), in_=hi1[:, lo:hi], func=COPY)
+        nc.scalar.activation(out=f2[:].indirect(idx6[:, 0:half]), in_=hi1[:], func=COPY)
+
+        d0_picks = sb.tile([P, PICKS], F32, tag="a_picks_then_d0_picks")
+        nc.vector.tensor_copy(out=d0_picks[:], in_=d0[:].indirect(idx4[:]))
+        c0 = sb.tile([P, T], F32, tag="d0_then_c0")
+        nc.vector.tensor_copy(out=c0[:, 0:BANK], in_=c0_lo)
+        nc.vector.tensor_copy(out=c0[:, BANK:T], in_=c0_hi)
+        c0_picks = sb.tile([P, PICKS], F32)
+        nc.vector.tensor_copy(out=c0_picks[:], in_=c0[:].indirect(idx3[:]))
         lo1 = sb.tile([P, PICKS], F32)
-        nc.vector.tensor_tensor(out=lo1[:], in0=gc[:], in1=gd[:], op=ALU.min)
-        nc.scalar.activation(out=f1[:].indirect(l5[:, cols:2 * cols]), in_=lo1[:], func=COPY)
-        nc.scalar.activation(out=f2[:].indirect(l6[:, cols:2 * cols]), in_=lo1[:], func=COPY)
+        nc.vector.tensor_tensor(out=lo1[:], in0=c0_picks[:], in1=d0_picks[:], op=ALU.min)
+        nc.scalar.activation(out=f1[:].indirect(idx5[:, half:2 * half]), in_=lo1[:], func=COPY)
+        nc.scalar.activation(out=f2[:].indirect(idx6[:, half:2 * half]), in_=lo1[:], func=COPY)
 
         aa = sb.tile([P, T], F32)
         bb = sb.tile([P, T], F32)
         nc.vector.tensor_tensor(out=aa[:], in0=a[:], in1=f1[:], op=ALU.subtract)
-        g7 = [sb.tile([P, PICKS], F32, name="g7_%d" % h) for h in range(2)]
-        g8 = [sb.tile([P, PICKS], F32, name="g8_%d" % h) for h in range(2)]
-        nc.vector.tensor_copy(out=g7[0][:], in_=aa[:].indirect(l7[:, 0:cols]))
-        nc.scalar.activation(out=g7[1][:], in_=aa[:].indirect(l7[:, cols:2 * cols]), func=COPY)
+        aa_slots = sb.tile([P, 2 * PICKS], F32)
+        nc.scalar.activation(out=aa_slots[:], in_=aa[:].indirect(idx7[:]), func=COPY)
         nc.vector.tensor_tensor(out=bb[:], in0=b[:], in1=f2[:], op=ALU.add)
-        nc.vector.tensor_copy(out=g8[0][:], in_=bb[:].indirect(l8[:, 0:cols]))
-        nc.scalar.activation(out=g8[1][:], in_=bb[:].indirect(l8[:, cols:2 * cols]), func=COPY)
+        bb_slots = [sb.tile([P, PICKS], F32, name="bb_slots%d" % h) for h in range(2)]
+        nc.vector.tensor_copy(out=bb_slots[0][:], in_=bb[:].indirect(idx8[:, 0:half]))
+        nc.scalar.activation(out=bb_slots[1][:], in_=bb[:].indirect(idx8[:, half:2 * half]), func=COPY)
         for h, queue in enumerate((nc.sync, nc.scalar)):
+            slots = slice(h * PICKS, (h + 1) * PICKS)
             y = sb.tile([P, PICKS], F32, name="y%d" % h)
-            nc.vector.tensor_tensor(out=y[:], in0=g7[h][:], in1=g8[h][:], op=ALU.min)
-            queue.dma_start(out=out[:, h * PICKS:(h + 1) * PICKS], in_=y[:])
+            nc.vector.tensor_tensor(out=y[:], in0=aa_slots[:, slots], in1=bb_slots[h][:], op=ALU.min)
+            queue.dma_start(out=out[:, slots], in_=y[:])

@@ -25,7 +25,7 @@ ROWS = 4
 PER_COL = 16
 FP8_FIRST = 4
 TAIL = T - BANK // 2
-LEAD = T // 16
+ADD_CUT = BANK + 192
 
 FLOPS = 4 * 2 * D * Q * T
 
@@ -37,6 +37,16 @@ def tile_attend_fourcourts_four_kernel(tc, query, cache_words, cache_scales, dra
     with ExitStack() as ctx:
         sb = ctx.enter_context(tc.tile_pool(name="sb", bufs=1))
         ps = ctx.enter_context(tc.psum_pool(name="ps", bufs=1))
+
+        def zeroed_folded_plane(name):
+            plane = sb.tile([P, 2 * T], U8, name=name, align_bytes=64)
+            nc.vector.memset(plane[:].bitcast(I32)[0:P // 2, :], 0)
+            return plane
+
+        def zeroed_direct_plane(name, engine):
+            plane = sb.tile([P, T], U8, name=name, align_bytes=64)
+            engine.memset(plane[:].bitcast(I32), 0)
+            return plane
 
         def load_folded_plane(plane, scales, first):
             src = scales[0].bitcast(I32).rearrange("(h u r) n -> u r h n", h=2, u=2, r=ROWS)
@@ -58,9 +68,10 @@ def tile_attend_fourcourts_four_kernel(tc, query, cache_words, cache_scales, dra
             nc.sync.dma_start(entries[:], src)
             return entries
 
-        def load_fp8_words(words, name):
-            codes = sb.tile([P, T], U32, name=name, align_bytes=64)
-            nc.sync.dma_start(out=codes[:].bitcast(I32), in_=words[0].rearrange("p n t -> p (n t)").bitcast(I32))
+        def load_fp8_words(words, lo, hi, name):
+            codes = sb.tile([P, hi - lo], U32, name=name, align_bytes=64)
+            src = words[0].rearrange("p n t -> p (n t)")[:, PACK * lo:PACK * hi].bitcast(I32)
+            nc.sync.dma_start(out=codes[:].bitcast(I32), in_=src)
             return codes
 
         def load_fp4_words(words, name):
@@ -68,34 +79,30 @@ def tile_attend_fourcourts_four_kernel(tc, query, cache_words, cache_scales, dra
             nc.sync.dma_start(out=codes[:].bitcast(I32), in_=words[0].bitcast(I32))
             return codes
 
-        draft_plane = sb.tile([P, 2 * T], U8, align_bytes=64)
-        cache_plane = sb.tile([P, 2 * T], U8, align_bytes=64)
-        pref_plane = sb.tile([P, T], U8, align_bytes=64)
-        arch_plane = sb.tile([P, T], U8, align_bytes=64)
+        draft_plane = zeroed_folded_plane("draft_plane")
+        cache_plane = zeroed_folded_plane("cache_plane")
+        pref_plane = zeroed_direct_plane("pref_plane", nc.vector)
         f1 = sb.tile([P, T], F32)
-        nc.vector.memset(draft_plane[:].bitcast(I32)[0:P // 2, :], 0)
-        nc.vector.memset(cache_plane[:].bitcast(I32)[0:P // 2, 0:T // 4], 0)
-        nc.gpsimd.memset(cache_plane[:].bitcast(I32)[0:P // 2, T // 4:T // 2], 0)
-        nc.gpsimd.memset(arch_plane[:].bitcast(I32), 0)
-        nc.vector.memset(pref_plane[:].bitcast(I32), 0)
         nc.vector.memset(f1[:], 0.0)
+        arch_plane = zeroed_direct_plane("arch_plane", nc.gpsimd)
 
         load_direct_plane(arch_plane, arch_scales, FP8_FIRST, nc.gpsimd)
         q_raw = sb.tile([P, PACK, Q], F32)
         nc.sync.dma_start(out=q_raw[:], in_=query.rearrange("(p t) w -> p t w", t=PACK))
         draft_codes = load_fp4_words(draft_words, "draft_codes")
         load_folded_plane(draft_plane, draft_scales, 0)
-        idx2 = load_list(offs2, "idx2")
         load_folded_plane(cache_plane, cache_scales, FP8_FIRST)
-        cache_codes = load_fp8_words(cache_words, "cache_codes")
+        cache_lo = load_fp8_words(cache_words, 0, BANK, "cache_lo")
+        cache_hi = load_fp8_words(cache_words, BANK, T, "cache_hi")
         pref_codes = load_fp4_words(pref_words, "pref_codes")
-        load_direct_plane(pref_plane, pref_scales, 0, nc.sync)
+        idx2 = load_list(offs2, "idx2")
         idx = load_list(offs, "idx")
-        arch_codes = load_fp8_words(arch_words, "arch_codes")
+        load_direct_plane(pref_plane, pref_scales, 0, nc.sync)
+        arch_codes = load_fp8_words(arch_words, 0, T, "arch_codes")
         idx5 = load_list(offs5, "idx5")
         idx4 = load_list(offs4, "idx4")
-        idx6 = load_list(offs6, "idx6")
         idx3 = load_list(offs3, "idx3")
+        idx6 = load_list(offs6, "idx6")
         idx7 = load_list(offs7, "idx7")
         idx8 = load_list(offs8, "idx8")
 
@@ -110,7 +117,7 @@ def tile_attend_fourcourts_four_kernel(tc, query, cache_words, cache_scales, dra
                               in_=q_bf[:].rearrange("p w t -> p (w t)"))
         unfold_plane(cache_plane)
         f2 = sb.tile([P, T], F32, tag="q_bf_then_f2", align_bytes=64)
-        nc.gpsimd.memset(f2[:], 0.0)
+        nc.vector.memset(f2[:], 0.0)
 
         def score(bank_tag, keys, key_scales):
             bank = ps.tile([P, BANK], F32, name=bank_tag, tag=bank_tag)
@@ -123,46 +130,41 @@ def tile_attend_fourcourts_four_kernel(tc, query, cache_words, cache_scales, dra
             return score(bank_tag, codes[:, 2 * lo:2 * hi].bitcast(FP4X4), plane[:, lo:hi])
 
         def score_fp8(bank_tag, codes, plane, lo, hi):
-            return score(bank_tag, codes[:, lo:hi].bitcast(FP8X4), plane[FP8_FIRST:P, lo:hi])
+            return score(bank_tag, codes.bitcast(FP8X4), plane[FP8_FIRST:P, lo:hi])
 
         a = sb.tile([P, T], F32)
         b = sb.tile([P, T], F32)
         b_lo = score_fp4("bank0", draft_codes, draft_plane, 0, BANK)
-        b_mid = score_fp4("bank1", draft_codes, draft_plane, BANK, TAIL)
-        b_tail = score_fp4("bank2", draft_codes, draft_plane, TAIL, T)
-        a_lo = score_fp8("bank3", cache_codes, cache_plane, 0, BANK)
-        a_mid = score_fp8("bank4", cache_codes, cache_plane, BANK, TAIL)
-        a_tail = score_fp8("bank5", cache_codes, cache_plane, TAIL, T)
+        b_hi = score_fp4("bank1", draft_codes, draft_plane, BANK, T)
+        a_lo = score_fp8("bank2", cache_lo[:, 0:BANK], cache_plane, 0, BANK)
+        a_mid = score_fp8("bank3", cache_hi[:, 0:TAIL - BANK], cache_plane, BANK, TAIL)
+        a_tail = score_fp8("bank4", cache_hi[:, TAIL - BANK:T - BANK], cache_plane, TAIL, T)
         nc.scalar.copy(out=b[:, 0:BANK], in_=b_lo)
-        nc.vector.tensor_copy(out=b[:, BANK:TAIL], in_=b_mid)
-        nc.vector.tensor_copy(out=b[:, TAIL:T], in_=b_tail)
-        b_picks = sb.tile([P, PICKS], F32)
-        nc.vector.tensor_copy(out=b_picks[:], in_=b[:].indirect(idx2[:]))
+        nc.vector.tensor_copy(out=b[:, BANK:T], in_=b_hi)
         nc.scalar.copy(out=a[:, 0:BANK], in_=a_lo)
+        b_picks = sb.tile([P, PICKS], F32, tag="b_picks_then_c0")
+        nc.vector.tensor_copy(out=b_picks[:], in_=b[:].indirect(idx2[:]))
         nc.scalar.copy(out=a[:, BANK:TAIL], in_=a_mid)
         nc.vector.tensor_copy(out=a[:, TAIL:T], in_=a_tail)
-        a_picks = sb.tile([P, PICKS], F32, tag="a_picks_then_d0_picks")
+        a_picks = sb.tile([P, PICKS], F32)
         nc.vector.tensor_copy(out=a_picks[:], in_=a[:].indirect(idx[:]))
         hi1 = sb.tile([P, PICKS], F32)
-        pieces = ((0, LEAD), (LEAD, PICKS))
-        for lo, hi in pieces:
-            nc.vector.tensor_tensor(out=hi1[:, lo:hi], in0=a_picks[:, lo:hi], in1=b_picks[:, lo:hi], op=ALU.max)
+        nc.vector.tensor_tensor(out=hi1[:], in0=a_picks[:], in1=b_picks[:], op=ALU.max)
 
-        d0 = sb.tile([P, T], F32, tag="d0_then_c0")
-        d0_lo = score_fp4("bank6", pref_codes, pref_plane, 0, BANK)
-        d0_hi = score_fp4("bank7", pref_codes, pref_plane, BANK, T)
-        c0_lo = score_fp8("bank3", arch_codes, arch_plane, 0, BANK)
-        c0_hi = score_fp8("bank4", arch_codes, arch_plane, BANK, T)
+        c0 = sb.tile([P, T], F32, tag="b_picks_then_c0")
+        d0 = sb.tile([P, T], F32)
+        d0_lo = score_fp4("bank5", pref_codes, pref_plane, 0, BANK)
+        d0_hi = score_fp4("bank6", pref_codes, pref_plane, BANK, T)
+        c0_lo = score_fp8("bank7", arch_codes[:, 0:BANK], arch_plane, 0, BANK)
+        c0_hi = score_fp8("bank2", arch_codes[:, BANK:T], arch_plane, BANK, T)
         nc.scalar.copy(out=d0[:, 0:BANK], in_=d0_lo)
         nc.scalar.copy(out=d0[:, BANK:T], in_=d0_hi)
-        half = PICKS // PER_COL
-        for lo, hi in pieces:
-            nc.scalar.activation(out=f1[:].indirect(idx5[:, lo // PER_COL:hi // PER_COL]), in_=hi1[:, lo:hi], func=COPY)
-        nc.scalar.activation(out=f2[:].indirect(idx6[:, 0:half]), in_=hi1[:], func=COPY)
 
-        d0_picks = sb.tile([P, PICKS], F32, tag="a_picks_then_d0_picks")
+        half = PICKS // PER_COL
+        nc.scalar.activation(out=f1[:].indirect(idx5[:, 0:half]), in_=hi1[:], func=COPY)
+        nc.scalar.activation(out=f2[:].indirect(idx6[:, 0:half]), in_=hi1[:], func=COPY)
+        d0_picks = sb.tile([P, PICKS], F32)
         nc.vector.tensor_copy(out=d0_picks[:], in_=d0[:].indirect(idx4[:]))
-        c0 = sb.tile([P, T], F32, tag="d0_then_c0")
         nc.vector.tensor_copy(out=c0[:, 0:BANK], in_=c0_lo)
         nc.vector.tensor_copy(out=c0[:, BANK:T], in_=c0_hi)
         c0_picks = sb.tile([P, PICKS], F32)
@@ -177,7 +179,10 @@ def tile_attend_fourcourts_four_kernel(tc, query, cache_words, cache_scales, dra
         nc.vector.tensor_tensor(out=aa[:], in0=a[:], in1=f1[:], op=ALU.subtract)
         aa_slots = sb.tile([P, 2 * PICKS], F32)
         nc.scalar.activation(out=aa_slots[:], in_=aa[:].indirect(idx7[:]), func=COPY)
-        nc.vector.tensor_tensor(out=bb[:], in0=b[:], in1=f2[:], op=ALU.add)
+        nc.vector.tensor_tensor(out=bb[:, 0:BANK], in0=b_lo, in1=f2[:, 0:BANK], op=ALU.add)
+        nc.vector.tensor_tensor(out=bb[:, BANK:ADD_CUT], in0=b_hi[:, 0:ADD_CUT - BANK], in1=f2[:, BANK:ADD_CUT],
+                                op=ALU.add)
+        nc.gpsimd.tensor_tensor(out=bb[:, ADD_CUT:T], in0=b[:, ADD_CUT:T], in1=f2[:, ADD_CUT:T], op=ALU.add)
         bb_slots = [sb.tile([P, PICKS], F32, name="bb_slots%d" % h) for h in range(2)]
         nc.vector.tensor_copy(out=bb_slots[0][:], in_=bb[:].indirect(idx8[:, 0:half]))
         nc.scalar.activation(out=bb_slots[1][:], in_=bb[:].indirect(idx8[:, half:2 * half]), func=COPY)

from contextlib import ExitStack

import concourse.mybir as mybir

F32 = mybir.dt.float32
BF16 = mybir.dt.bfloat16
I32 = mybir.dt.int32
U32 = mybir.dt.uint32
U16 = mybir.dt.uint16
U8 = mybir.dt.uint8
FP8X4 = mybir.dt.float8_e4m3fn_x4
FP4X4 = mybir.dt.float4_e2m1fn_x4
ALU = mybir.AluOpType
COPY = mybir.ActivationFunctionType.Copy

P = 128
PACK = 4
D = P * PACK
Q = 128
T = 1024
PICKS = 256
BANK = 512
QUAD = 32
ROWS = 4
PER_COL = 16
FP8_FIRST = 4
TAIL = T - BANK // 2
ADD_CUT = BANK + 192

FLOPS = 4 * 2 * D * Q * T


def tile_attend_fourcourts_four_kernel(tc, query, cache_words, cache_scales, draft_words, draft_scales,
                                        arch_words, arch_scales, pref_words, pref_scales,
                                        offs, offs2, offs3, offs4, offs5, offs6, offs7, offs8, out):
    nc = tc.nc
    with ExitStack() as ctx:
        sb = ctx.enter_context(tc.tile_pool(name="sb", bufs=1))
        ps = ctx.enter_context(tc.psum_pool(name="ps", bufs=1))

        def zeroed_folded_plane(name):
            plane = sb.tile([P, 2 * T], U8, name=name, align_bytes=64)
            nc.vector.memset(plane[:].bitcast(I32)[0:P // 2, :], 0)
            return plane

        def zeroed_direct_plane(name, engine):
            plane = sb.tile([P, T], U8, name=name, align_bytes=64)
            engine.memset(plane[:].bitcast(I32), 0)
            return plane

        def load_folded_plane(plane, scales, first):
            src = scales[0].bitcast(I32).rearrange("(h u r) n -> u r h n", h=2, u=2, r=ROWS)
            dst = plane[:].bitcast(I32).rearrange("p (h n) -> p h n", h=2)
            for u in range(2):
                nc.sync.dma_start(out=dst[QUAD * u + first:QUAD * u + first + ROWS], in_=src[u])

        def unfold_plane(plane):
            as_i32 = plane[:].bitcast(I32)
            nc.vector.tensor_copy(out=as_i32[P // 2:P, 0:T // 4], in_=as_i32[0:P // 2, T // 4:T // 2])

        def load_direct_plane(plane, scales, first, queue):
            src = scales[0].bitcast(I32).rearrange("(u r) n -> r u n", r=ROWS)
            for r in range(ROWS):
                queue.dma_start(out=plane[:].bitcast(I32)[first + r:P:QUAD, :], in_=src[r])

        def load_list(src, name):
            entries = sb.tile([P, src.shape[1]], U16, name=name)
            nc.sync.dma_start(entries[:], src)
            return entries

        def load_fp8_words(words, lo, hi, name):
            codes = sb.tile([P, hi - lo], U32, name=name, align_bytes=64)
            src = words[0].rearrange("p n t -> p (n t)")[:, PACK * lo:PACK * hi].bitcast(I32)
            nc.sync.dma_start(out=codes[:].bitcast(I32), in_=src)
            return codes

        def load_fp4_words(words, name):
            codes = sb.tile([P, 2 * T], U8, name=name, align_bytes=64)
            nc.sync.dma_start(out=codes[:].bitcast(I32), in_=words[0].bitcast(I32))
            return codes

        draft_plane = zeroed_folded_plane("draft_plane")
        cache_plane = zeroed_folded_plane("cache_plane")
        pref_plane = zeroed_direct_plane("pref_plane", nc.vector)
        f1 = sb.tile([P, T], F32)
        nc.vector.memset(f1[:], 0.0)
        arch_plane = zeroed_direct_plane("arch_plane", nc.gpsimd)

        load_direct_plane(arch_plane, arch_scales, FP8_FIRST, nc.gpsimd)
        q_raw = sb.tile([P, PACK, Q], F32)
        nc.sync.dma_start(out=q_raw[:], in_=query.rearrange("(p t) w -> p t w", t=PACK))
        draft_codes = load_fp4_words(draft_words, "draft_codes")
        load_folded_plane(draft_plane, draft_scales, 0)
        load_folded_plane(cache_plane, cache_scales, FP8_FIRST)
        cache_lo = load_fp8_words(cache_words, 0, BANK, "cache_lo")
        cache_hi = load_fp8_words(cache_words, BANK, T, "cache_hi")
        pref_codes = load_fp4_words(pref_words, "pref_codes")
        idx2 = load_list(offs2, "idx2")
        idx = load_list(offs, "idx")
        load_direct_plane(pref_plane, pref_scales, 0, nc.sync)
        arch_codes = load_fp8_words(arch_words, 0, T, "arch_codes")
        idx5 = load_list(offs5, "idx5")
        idx4 = load_list(offs4, "idx4")
        idx3 = load_list(offs3, "idx3")
        idx6 = load_list(offs6, "idx6")
        idx7 = load_list(offs7, "idx7")
        idx8 = load_list(offs8, "idx8")

        q_bf = sb.tile([P, Q, PACK], BF16, tag="q_bf_then_f2", align_bytes=64)
        q_by_col = q_raw[:].rearrange("p t w -> p w t")
        nc.scalar.activation(out=q_bf[:, 0:Q // 2, :], in_=q_by_col[:, 0:Q // 2, :], func=COPY)
        nc.vector.tensor_copy(out=q_bf[:, Q // 2:Q, :], in_=q_by_col[:, Q // 2:Q, :])
        unfold_plane(draft_plane)
        q_codes = sb.tile([P, Q], U32, align_bytes=64)
        q_plane = sb.tile([P, Q], U8, align_bytes=64)
        nc.vector.quantize_mx(out=q_codes[:].bitcast(FP8X4), scales=q_plane[:],
                              in_=q_bf[:].rearrange("p w t -> p (w t)"))
        unfold_plane(cache_plane)
        f2 = sb.tile([P, T], F32, tag="q_bf_then_f2", align_bytes=64)
        nc.vector.memset(f2[:], 0.0)

        def score(bank_tag, keys, key_scales):
            bank = ps.tile([P, BANK], F32, name=bank_tag, tag=bank_tag)
            scores = bank[:, 0:key_scales.shape[1]]
            nc.tensor.matmul_mx(out=scores, lhsT=q_codes[:].bitcast(FP8X4), lhsT_scale=q_plane[:],
                                rhs=keys, rhs_scale=key_scales, start=True, stop=True)
            return scores

        def score_fp4(bank_tag, codes, plane, lo, hi):
            return score(bank_tag, codes[:, 2 * lo:2 * hi].bitcast(FP4X4), plane[:, lo:hi])

        def score_fp8(bank_tag, codes, plane, lo, hi):
            return score(bank_tag, codes.bitcast(FP8X4), plane[FP8_FIRST:P, lo:hi])

        a = sb.tile([P, T], F32)
        b = sb.tile([P, T], F32)
        b_lo = score_fp4("bank0", draft_codes, draft_plane, 0, BANK)
        b_hi = score_fp4("bank1", draft_codes, draft_plane, BANK, T)
        a_lo = score_fp8("bank2", cache_lo[:, 0:BANK], cache_plane, 0, BANK)
        a_mid = score_fp8("bank3", cache_hi[:, 0:TAIL - BANK], cache_plane, BANK, TAIL)
        a_tail = score_fp8("bank4", cache_hi[:, TAIL - BANK:T - BANK], cache_plane, TAIL, T)
        nc.scalar.copy(out=b[:, 0:BANK], in_=b_lo)
        nc.vector.tensor_copy(out=b[:, BANK:T], in_=b_hi)
        nc.scalar.copy(out=a[:, 0:BANK], in_=a_lo)
        b_picks = sb.tile([P, PICKS], F32, tag="b_picks_then_c0")
        nc.vector.tensor_copy(out=b_picks[:], in_=b[:].indirect(idx2[:]))
        nc.scalar.copy(out=a[:, BANK:TAIL], in_=a_mid)
        nc.vector.tensor_copy(out=a[:, TAIL:T], in_=a_tail)
        a_picks = sb.tile([P, PICKS], F32)
        nc.vector.tensor_copy(out=a_picks[:], in_=a[:].indirect(idx[:]))
        hi1 = sb.tile([P, PICKS], F32)
        nc.vector.tensor_tensor(out=hi1[:], in0=a_picks[:], in1=b_picks[:], op=ALU.max)

        c0 = sb.tile([P, T], F32, tag="b_picks_then_c0")
        d0 = sb.tile([P, T], F32)
        d0_lo = score_fp4("bank5", pref_codes, pref_plane, 0, BANK)
        d0_hi = score_fp4("bank6", pref_codes, pref_plane, BANK, T)
        c0_lo = score_fp8("bank7", arch_codes[:, 0:BANK], arch_plane, 0, BANK)
        c0_hi = score_fp8("bank2", arch_codes[:, BANK:T], arch_plane, BANK, T)
        nc.scalar.copy(out=d0[:, 0:BANK], in_=d0_lo)
        nc.scalar.copy(out=d0[:, BANK:T], in_=d0_hi)

        half = PICKS // PER_COL
        nc.scalar.activation(out=f1[:].indirect(idx5[:, 0:half]), in_=hi1[:], func=COPY)
        nc.scalar.activation(out=f2[:].indirect(idx6[:, 0:half]), in_=hi1[:], func=COPY)
        d0_picks = sb.tile([P, PICKS], F32)
        nc.vector.tensor_copy(out=d0_picks[:], in_=d0[:].indirect(idx4[:]))
        nc.vector.tensor_copy(out=c0[:, 0:BANK], in_=c0_lo)
        nc.vector.tensor_copy(out=c0[:, BANK:T], in_=c0_hi)
        c0_picks = sb.tile([P, PICKS], F32)
        nc.vector.tensor_copy(out=c0_picks[:], in_=c0[:].indirect(idx3[:]))
        lo1 = sb.tile([P, PICKS], F32)
        nc.vector.tensor_tensor(out=lo1[:], in0=c0_picks[:], in1=d0_picks[:], op=ALU.min)
        nc.scalar.activation(out=f1[:].indirect(idx5[:, half:2 * half]), in_=lo1[:], func=COPY)
        nc.scalar.activation(out=f2[:].indirect(idx6[:, half:2 * half]), in_=lo1[:], func=COPY)

        aa = sb.tile([P, T], F32)
        bb = sb.tile([P, T], F32)
        nc.vector.tensor_tensor(out=aa[:], in0=a[:], in1=f1[:], op=ALU.subtract)
        aa_slots = sb.tile([P, 2 * PICKS], F32)
        nc.scalar.activation(out=aa_slots[:], in_=aa[:].indirect(idx7[:]), func=COPY)
        nc.vector.tensor_tensor(out=bb[:, 0:BANK], in0=b_lo, in1=f2[:, 0:BANK], op=ALU.add)
        nc.vector.tensor_tensor(out=bb[:, BANK:ADD_CUT], in0=b_hi[:, 0:ADD_CUT - BANK], in1=f2[:, BANK:ADD_CUT],
                                op=ALU.add)
        nc.gpsimd.tensor_tensor(out=bb[:, ADD_CUT:T], in0=b[:, ADD_CUT:T], in1=f2[:, ADD_CUT:T], op=ALU.add)
        bb_slots = [sb.tile([P, PICKS], F32, name="bb_slots%d" % h) for h in range(2)]
        nc.vector.tensor_copy(out=bb_slots[0][:], in_=bb[:].indirect(idx8[:, 0:half]))
        nc.scalar.activation(out=bb_slots[1][:], in_=bb[:].indirect(idx8[:, half:2 * half]), func=COPY)
        for h, queue in enumerate((nc.sync, nc.scalar)):
            slots = slice(h * PICKS, (h + 1) * PICKS)
            y = sb.tile([P, PICKS], F32, name="y%d" % h)
            nc.vector.tensor_tensor(out=y[:], in0=aa_slots[:, slots], in1=bb_slots[h][:], op=ALU.min)
            queue.dma_start(out=out[:, slots], in_=y[:])
